import numpy as np, ml_dtypes
CORES = [9,41,49,65,73,81,97,113,15,47,55,71,79,87,103,119]
N = 16
KT, HT, TK = 4, 1, 128
def setup_inputs(rng):
    w = (rng.standard_normal((128, KT * HT * 128), dtype=np.float32) / 8).astype(ml_dtypes.bfloat16)
    return {"x": rng.standard_normal((N, 128, KT * TK), dtype=np.float32).astype(ml_dtypes.bfloat16), "w": np.broadcast_to(w, (N,) + w.shape).copy()}
def setup_inputs_big(rng):
    d = setup_inputs(rng)
    for k in ("x", "w"): d[k] = (d[k].astype(np.float32) * 1024.0).astype(d[k].dtype)
    return d
def setup_inputs_small(rng):
    d = setup_inputs(rng)
    for k in ("x", "w"): d[k] = (d[k].astype(np.float32) * (1 / 1024.0)).astype(d[k].dtype)
    return d
def setup_inputs_apart(rng):
    d = setup_inputs(rng)
    f = (10.0 ** rng.permutation(np.linspace(-1.5, 1.5, N))).astype(np.float32).reshape(N, 1, 1)
    for k in ("x",): d[k] = (d[k].astype(np.float32) * f).astype(d[k].dtype)
    return d
def tie_inputs(x):
    x = dict(x)
    x["w"] = np.broadcast_to(x["w"][0], x["w"].shape).copy()
    return x
def reference(x, w):
    X, W = x.astype(np.float64), w.astype(np.float64)
    def hidden(r):
        return np.stack([np.maximum(sum(W[r][:, 128 * (HT * t + u):128 * (HT * t + u) + 128].T @ X[r][:, TK * t:TK * t + TK] for t in range(KT)), 0.0) for u in range(HT)])
    h = [hidden(r) for r in range(N)]
    y = np.stack([sum(h[(r - 1) % N][u].T @ h[r][u] for u in range(HT)) for r in range(N)])
    return {"y": y.astype(ml_dtypes.bfloat16 if x.dtype != np.float64 else np.float64)}

@@ -1,0 +1,92 @@
+from concourse.mybir import AluOpType
+
+TILE = 128
+KT = 4
+LANES = 8
+
+SCRATCH = {
+    "xs": ("sbuf", [128, KT * TILE], "bfloat16"),
+    "ws": ("sbuf", [128, KT * TILE], "bfloat16"),
+    "zero": ("sbuf", [128, TILE], "float32"),
+    "h": ("sbuf", [128, TILE], "bfloat16"),
+    "hp": ("sbuf", [128, TILE], "bfloat16"),
+    "fwd": ("sbuf", [128, TILE], "bfloat16"),
+    "ys": ("sbuf", [128, TILE], "bfloat16"),
+    "ph": ("psum", [128, 512], "float32"),
+    "py": ("psum", [128, 512], "float32"),
+}
+SEMAPHORES = ["loaded", "zeroed", "summed", "hready", "passed", "arrived", "sent", "multiplied", "rounded", "stored"]
+
+
+def _lanes(topo, src, dst):
+    allowed = topo.mask(src, dst)
+    bits = [1 << b for b in range(allowed.bit_length()) if (allowed >> b) & 1]
+    chosen = bits[::max(1, len(bits) // LANES)][:LANES]
+    return sum(chosen), len(chosen)
+
+
+def _via(T, topo, src, dst):
+    if topo.may_write(src, dst):
+        return None
+    able = [c for c in range(topo.CHIPS * topo.CORES_PER_CHIP)
+            if c != src and c != dst and topo.chip(c) == topo.chip(src) and topo.may_write(c, dst)]
+    ranks = [c for c in able if T.rank_of(c) is not None]
+    return (ranks or able)[0]
+
+
+def _send(g, T, topo, src, dst, out, in_, sem):
+    rid, pid, _ = topo.addr(dst)
+    mask, count = _lanes(topo, src, dst)
+    g.remote_dma(out_ap=out, in_ap=in_, remote_sem=sem, local_sem=T.sem.sent, pid=pid, routing_id=rid,
+                 dma_engine_mask=mask)
+    return count
+
+
+def rank_program(g, core, T, topo):
+    cores = list(T.cores)
+    n = len(cores)
+    edges = [(cores[r], _via(T, topo, cores[r], cores[(r + 1) % n]), cores[(r + 1) % n]) for r in range(n)]
+    passing = [(s, d) for (s, v, d) in edges if v == core]
+    rank = T.rank_of(core)
+    if rank is None and not passing:
+        return
+    S = T.sem
+    sent = 0
+
+    if rank is not None:
+        g.sync.dma_start(T.xs[:], T.x[:]).then_inc(S.loaded, 16)
+        g.scalar.dma_start(T.ws[:], T.w[:]).then_inc(S.loaded, 16)
+        g.vector.memset(T.zero[:], 0.0).then_inc(S.zeroed, 1)
+
+        g.tensor.wait_ge(S.loaded, 32)
+        for t in range(KT):
+            cols = slice(t * TILE, (t + 1) * TILE)
+            mm = g.tensor.matmul(T.ph[:, 0:TILE], T.ws[:, cols], T.xs[:, cols], start=(t == 0), stop=(t == KT - 1))
+        mm.then_inc(S.summed, 1)
+        g.vector.wait_ge(S.zeroed, 1)
+        g.vector.wait_ge(S.summed, 1)
+        g.vector.tensor_tensor(T.h[:], T.ph[:, 0:TILE], T.zero[:], AluOpType.max).then_inc(S.hready, 1)
+
+        _, via, nxt = edges[rank]
+        g.wait_ge(S.hready, 1)
+        if via is None:
+            sent += _send(g, T, topo, core, nxt, T.hp[:], T.h[:], S.arrived)
+        else:
+            sent += _send(g, T, topo, core, via, T.fwd[:], T.h[:], S.passed)
+
+    for (src, dst) in passing:
+        g.wait_ge(S.passed, _lanes(topo, src, core)[1])
+        sent += _send(g, T, topo, core, dst, T.hp[:], T.fwd[:], S.arrived)
+
+    if rank is not None:
+        src, via, _ = edges[(rank - 1) % n]
+        g.tensor.wait_ge(S.hready, 1)
+        g.tensor.wait_ge(S.arrived, _lanes(topo, src if via is None else via, core)[1])
+        g.tensor.matmul(T.py[:, 0:TILE], T.hp[:], T.h[:], start=True, stop=True).then_inc(S.multiplied, 1)
+        g.vector.wait_ge(S.multiplied, 1)
+        g.vector.tensor_copy(T.ys[:], T.py[:, 0:TILE]).then_inc(S.rounded, 1)
+        g.sync.wait_ge(S.rounded, 1)
+        g.sync.dma_start(T.y[:], T.ys[:]).then_inc(S.stored, 16)
+        g.sync.wait_ge(S.stored, 16)
+
+    g.wait_ge(S.sent, sent)

@@ -2,7 +2,8 @@ from concourse.mybir import AluOpType
 
 TILE = 128
 KT = 4
-LANES = 8
+HALF = TILE // 2
+HALVES = ("a", "b")
 
 SCRATCH = {
     "xs": ("sbuf", [128, KT * TILE], "bfloat16"),
@@ -10,28 +11,37 @@ SCRATCH = {
     "zero": ("sbuf", [128, TILE], "float32"),
     "h": ("sbuf", [128, TILE], "bfloat16"),
     "hp": ("sbuf", [128, TILE], "bfloat16"),
-    "fwd": ("sbuf", [128, TILE], "bfloat16"),
+    "sp": ("sbuf", [128, TILE], "bfloat16"),
+    "x0n": ("sbuf", [128, TILE], "bfloat16"),
+    "spn": ("sbuf", [128, TILE], "bfloat16"),
+    "hn": ("sbuf", [128, TILE], "bfloat16"),
+    "ones": ("sbuf", [128, TILE], "bfloat16"),
+    "eye": ("sbuf", [128, TILE], "bfloat16"),
     "ys": ("sbuf", [128, TILE], "bfloat16"),
     "ph": ("psum", [128, 512], "float32"),
-    "py": ("psum", [128, 512], "float32"),
+    "pya": ("psum", [128, 512], "float32"),
+    "pyb": ("psum", [128, 512], "float32"),
+    "ppa": ("psum", [128, 512], "float32"),
+    "ppb": ("psum", [128, 512], "float32"),
+    "pna": ("psum", [128, 512], "float32"),
+    "pnb": ("psum", [128, 512], "float32"),
 }
-SEMAPHORES = ["loaded", "zeroed", "summed", "hready", "passed", "arrived", "sent", "multiplied", "rounded", "stored"]
+SEMAPHORES = ["first", "loaded", "last", "zeroed", "filled", "cut", "partiala", "partialb", "spready", "summed", "hready",
+              "early", "passed", "finisheda", "finishedb", "hnready", "arrived", "sent", "multiplieda", "multipliedb",
+              "rounded", "stored"]
 
 
 def _lanes(topo, src, dst):
     allowed = topo.mask(src, dst)
     bits = [1 << b for b in range(allowed.bit_length()) if (allowed >> b) & 1]
-    chosen = bits[::max(1, len(bits) // LANES)][:LANES]
-    return sum(chosen), len(chosen)
+    return sum(bits), len(bits)
 
 
 def _via(T, topo, src, dst):
     if topo.may_write(src, dst):
         return None
-    able = [c for c in range(topo.CHIPS * topo.CORES_PER_CHIP)
-            if c != src and c != dst and topo.chip(c) == topo.chip(src) and topo.may_write(c, dst)]
-    ranks = [c for c in able if T.rank_of(c) is not None]
-    return (ranks or able)[0]
+    able = [c for c in T.cores if c != src and c != dst and topo.chip(c) == topo.chip(src) and topo.may_write(c, dst)]
+    return able[0]
 
 
 def _send(g, T, topo, src, dst, out, in_, sem):
@@ -42,51 +52,93 @@ def _send(g, T, topo, src, dst, out, in_, sem):
     return count
 
 
+def _tile(t):
+    return slice(t * TILE, (t + 1) * TILE)
+
+
+def _half(i, t=0):
+    return slice(t * TILE + i * HALF, t * TILE + (i + 1) * HALF)
+
+
 def rank_program(g, core, T, topo):
     cores = list(T.cores)
     n = len(cores)
+    rank = T.rank_of(core)
+    if rank is None:
+        return
     edges = [(cores[r], _via(T, topo, cores[r], cores[(r + 1) % n]), cores[(r + 1) % n]) for r in range(n)]
     passing = [(s, d) for (s, v, d) in edges if v == core]
-    rank = T.rank_of(core)
-    if rank is None and not passing:
-        return
+    _, via, nxt = edges[rank]
     S = T.sem
     sent = 0
 
-    if rank is not None:
+    if via is None:
         g.sync.dma_start(T.xs[:], T.x[:]).then_inc(S.loaded, 16)
         g.scalar.dma_start(T.ws[:], T.w[:]).then_inc(S.loaded, 16)
-        g.vector.memset(T.zero[:], 0.0).then_inc(S.zeroed, 1)
+    else:
+        g.sync.dma_start(T.xs[:, _tile(0)], T.x[:, _tile(0)]).then_inc(S.first, 16)
+        g.sync.dma_start(T.xs[:, TILE:], T.x[:, TILE:]).then_inc(S.loaded, 16)
+        g.sync.dma_start(T.ws[:, TILE:], T.w[:, TILE:]).then_inc(S.loaded, 16)
+        g.sync.dma_start(T.ws[:, _tile(0)], T.w[:, _tile(0)]).then_inc(S.last, 16)
+    g.vector.memset(T.zero[:], 0.0).then_inc(S.zeroed, 1)
+    g.vector.wait_ge(S.zeroed, 1)
 
-        g.tensor.wait_ge(S.loaded, 32)
-        for t in range(KT):
-            cols = slice(t * TILE, (t + 1) * TILE)
-            mm = g.tensor.matmul(T.ph[:, 0:TILE], T.ws[:, cols], T.xs[:, cols], start=(t == 0), stop=(t == KT - 1))
-        mm.then_inc(S.summed, 1)
-        g.vector.wait_ge(S.zeroed, 1)
-        g.vector.wait_ge(S.summed, 1)
-        g.vector.tensor_tensor(T.h[:], T.ph[:, 0:TILE], T.zero[:], AluOpType.max).then_inc(S.hready, 1)
+    if passing:
+        g.vector.memset(T.ones[:], 1.0).then_inc(S.filled, 1)
+        g.wait_ge(S.filled, 1)
+        g.affine_select(T.eye[:], T.ones[:], [[-1, TILE]], AluOpType.is_equal, 0.0, 0, 1).then_inc(S.cut, 1)
 
-        _, via, nxt = edges[rank]
+    g.tensor.wait_ge(S.loaded, 32)
+    if via is not None:
+        g.wait_ge(S.first, 16)
+        sent += _send(g, T, topo, core, via, T.x0n[:], T.xs[:, _tile(0)], S.early)
+        for i, c in enumerate(HALVES):
+            for t in range(1, KT):
+                mm = g.tensor.matmul(T["pp" + c][:, 0:HALF], T.ws[:, _tile(t)], T.xs[:, _half(i, t)],
+                                     start=(t == 1), stop=(t == KT - 1))
+            mm.then_inc(S["partial" + c], 1)
+            g.vector.wait_ge(S["partial" + c], 1)
+            g.vector.tensor_copy(T.sp[:, _half(i)], T["pp" + c][:, 0:HALF]).then_inc(S.spready, 1)
+        g.wait_ge(S.spready, 2)
+        sent += _send(g, T, topo, core, via, T.spn[:], T.sp[:], S.passed)
+        g.tensor.wait_ge(S.first, 16)
+        g.tensor.wait_ge(S.last, 16)
+
+    for t in range(KT):
+        mm = g.tensor.matmul(T.ph[:, 0:TILE], T.ws[:, _tile(t)], T.xs[:, _tile(t)], start=(t == 0), stop=(t == KT - 1))
+    mm.then_inc(S.summed, 1)
+    g.vector.wait_ge(S.summed, 1)
+    g.vector.tensor_tensor(T.h[:], T.ph[:, 0:TILE], T.zero[:], AluOpType.max).then_inc(S.hready, 1)
+    if via is None:
         g.wait_ge(S.hready, 1)
-        if via is None:
-            sent += _send(g, T, topo, core, nxt, T.hp[:], T.h[:], S.arrived)
-        else:
-            sent += _send(g, T, topo, core, via, T.fwd[:], T.h[:], S.passed)
+        sent += _send(g, T, topo, core, nxt, T.hp[:], T.h[:], S.arrived)
 
     for (src, dst) in passing:
-        g.wait_ge(S.passed, _lanes(topo, src, core)[1])
-        sent += _send(g, T, topo, core, dst, T.hp[:], T.fwd[:], S.arrived)
+        lanes = _lanes(topo, src, core)[1]
+        g.tensor.wait_ge(S.early, lanes)
+        for i, c in enumerate(HALVES):
+            g.tensor.matmul(T["pn" + c][:, 0:HALF], T.ws[:, _tile(0)], T.x0n[:, _half(i)], start=True, stop=False)
+        g.tensor.wait_ge(S.cut, 1)
+        g.tensor.wait_ge(S.passed, lanes)
+        for i, c in enumerate(HALVES):
+            g.tensor.matmul(T["pn" + c][:, 0:HALF], T.eye[:], T.spn[:, _half(i)],
+                            start=False, stop=True).then_inc(S["finished" + c], 1)
+            g.vector.wait_ge(S["finished" + c], 1)
+            g.vector.tensor_tensor(T.hn[:, _half(i)], T["pn" + c][:, 0:HALF], T.zero[:, 0:HALF],
+                                   AluOpType.max).then_inc(S.hnready, 1)
+        g.wait_ge(S.hnready, 2)
+        sent += _send(g, T, topo, core, dst, T.hp[:], T.hn[:], S.arrived)
 
-    if rank is not None:
-        src, via, _ = edges[(rank - 1) % n]
-        g.tensor.wait_ge(S.hready, 1)
-        g.tensor.wait_ge(S.arrived, _lanes(topo, src if via is None else via, core)[1])
-        g.tensor.matmul(T.py[:, 0:TILE], T.hp[:], T.h[:], start=True, stop=True).then_inc(S.multiplied, 1)
-        g.vector.wait_ge(S.multiplied, 1)
-        g.vector.tensor_copy(T.ys[:], T.py[:, 0:TILE]).then_inc(S.rounded, 1)
-        g.sync.wait_ge(S.rounded, 1)
-        g.sync.dma_start(T.y[:], T.ys[:]).then_inc(S.stored, 16)
-        g.sync.wait_ge(S.stored, 16)
+    src, pvia, _ = edges[(rank - 1) % n]
+    g.tensor.wait_ge(S.hready, 1)
+    g.tensor.wait_ge(S.arrived, _lanes(topo, src if pvia is None else pvia, core)[1])
+    for i, c in enumerate(HALVES):
+        g.tensor.matmul(T["py" + c][:, 0:HALF], T.hp[:], T.h[:, _half(i)],
+                        start=True, stop=True).then_inc(S["multiplied" + c], 1)
+        g.vector.wait_ge(S["multiplied" + c], 1)
+        g.vector.tensor_copy(T.ys[:, _half(i)], T["py" + c][:, 0:HALF]).then_inc(S.rounded, 1)
+    g.sync.wait_ge(S.rounded, 2)
+    g.sync.dma_start(T.y[:], T.ys[:]).then_inc(S.stored, 16)
+    g.sync.wait_ge(S.stored, 16)
 
     g.wait_ge(S.sent, sent)

from concourse.mybir import AluOpType

TILE = 128
KT = 4
HALF = TILE // 2
HALVES = ("a", "b")

SCRATCH = {
    "xs": ("sbuf", [128, KT * TILE], "bfloat16"),
    "ws": ("sbuf", [128, KT * TILE], "bfloat16"),
    "zero": ("sbuf", [128, TILE], "float32"),
    "h": ("sbuf", [128, TILE], "bfloat16"),
    "hp": ("sbuf", [128, TILE], "bfloat16"),
    "sp": ("sbuf", [128, TILE], "bfloat16"),
    "x0n": ("sbuf", [128, TILE], "bfloat16"),
    "spn": ("sbuf", [128, TILE], "bfloat16"),
    "hn": ("sbuf", [128, TILE], "bfloat16"),
    "ones": ("sbuf", [128, TILE], "bfloat16"),
    "eye": ("sbuf", [128, TILE], "bfloat16"),
    "ys": ("sbuf", [128, TILE], "bfloat16"),
    "ph": ("psum", [128, 512], "float32"),
    "pya": ("psum", [128, 512], "float32"),
    "pyb": ("psum", [128, 512], "float32"),
    "ppa": ("psum", [128, 512], "float32"),
    "ppb": ("psum", [128, 512], "float32"),
    "pna": ("psum", [128, 512], "float32"),
    "pnb": ("psum", [128, 512], "float32"),
}
SEMAPHORES = ["first", "loaded", "last", "zeroed", "filled", "cut", "partiala", "partialb", "spready", "summed", "hready",
              "early", "passed", "finisheda", "finishedb", "hnready", "arrived", "sent", "multiplieda", "multipliedb",
              "rounded", "stored"]


def _lanes(topo, src, dst):
    allowed = topo.mask(src, dst)
    bits = [1 << b for b in range(allowed.bit_length()) if (allowed >> b) & 1]
    return sum(bits), len(bits)


def _via(T, topo, src, dst):
    if topo.may_write(src, dst):
        return None
    able = [c for c in T.cores if c != src and c != dst and topo.chip(c) == topo.chip(src) and topo.may_write(c, dst)]
    return able[0]


def _send(g, T, topo, src, dst, out, in_, sem):
    rid, pid, _ = topo.addr(dst)
    mask, count = _lanes(topo, src, dst)
    g.remote_dma(out_ap=out, in_ap=in_, remote_sem=sem, local_sem=T.sem.sent, pid=pid, routing_id=rid,
                 dma_engine_mask=mask)
    return count


def _tile(t):
    return slice(t * TILE, (t + 1) * TILE)


def _half(i, t=0):
    return slice(t * TILE + i * HALF, t * TILE + (i + 1) * HALF)


def rank_program(g, core, T, topo):
    cores = list(T.cores)
    n = len(cores)
    rank = T.rank_of(core)
    if rank is None:
        return
    edges = [(cores[r], _via(T, topo, cores[r], cores[(r + 1) % n]), cores[(r + 1) % n]) for r in range(n)]
    passing = [(s, d) for (s, v, d) in edges if v == core]
    _, via, nxt = edges[rank]
    S = T.sem
    sent = 0

    if via is None:
        g.sync.dma_start(T.xs[:], T.x[:]).then_inc(S.loaded, 16)
        g.scalar.dma_start(T.ws[:], T.w[:]).then_inc(S.loaded, 16)
    else:
        g.sync.dma_start(T.xs[:, _tile(0)], T.x[:, _tile(0)]).then_inc(S.first, 16)
        g.sync.dma_start(T.xs[:, TILE:], T.x[:, TILE:]).then_inc(S.loaded, 16)
        g.sync.dma_start(T.ws[:, TILE:], T.w[:, TILE:]).then_inc(S.loaded, 16)
        g.sync.dma_start(T.ws[:, _tile(0)], T.w[:, _tile(0)]).then_inc(S.last, 16)
    g.vector.memset(T.zero[:], 0.0).then_inc(S.zeroed, 1)
    g.vector.wait_ge(S.zeroed, 1)

    if passing:
        g.vector.memset(T.ones[:], 1.0).then_inc(S.filled, 1)
        g.wait_ge(S.filled, 1)
        g.affine_select(T.eye[:], T.ones[:], [[-1, TILE]], AluOpType.is_equal, 0.0, 0, 1).then_inc(S.cut, 1)

    g.tensor.wait_ge(S.loaded, 32)
    if via is not None:
        g.wait_ge(S.first, 16)
        sent += _send(g, T, topo, core, via, T.x0n[:], T.xs[:, _tile(0)], S.early)
        for i, c in enumerate(HALVES):
            for t in range(1, KT):
                mm = g.tensor.matmul(T["pp" + c][:, 0:HALF], T.ws[:, _tile(t)], T.xs[:, _half(i, t)],
                                     start=(t == 1), stop=(t == KT - 1))
            mm.then_inc(S["partial" + c], 1)
            g.vector.wait_ge(S["partial" + c], 1)
            g.vector.tensor_copy(T.sp[:, _half(i)], T["pp" + c][:, 0:HALF]).then_inc(S.spready, 1)
        g.wait_ge(S.spready, 2)
        sent += _send(g, T, topo, core, via, T.spn[:], T.sp[:], S.passed)
        g.tensor.wait_ge(S.first, 16)
        g.tensor.wait_ge(S.last, 16)

    for t in range(KT):
        mm = g.tensor.matmul(T.ph[:, 0:TILE], T.ws[:, _tile(t)], T.xs[:, _tile(t)], start=(t == 0), stop=(t == KT - 1))
    mm.then_inc(S.summed, 1)
    g.vector.wait_ge(S.summed, 1)
    g.vector.tensor_tensor(T.h[:], T.ph[:, 0:TILE], T.zero[:], AluOpType.max).then_inc(S.hready, 1)
    if via is None:
        g.wait_ge(S.hready, 1)
        sent += _send(g, T, topo, core, nxt, T.hp[:], T.h[:], S.arrived)

    for (src, dst) in passing:
        lanes = _lanes(topo, src, core)[1]
        g.tensor.wait_ge(S.early, lanes)
        for i, c in enumerate(HALVES):
            g.tensor.matmul(T["pn" + c][:, 0:HALF], T.ws[:, _tile(0)], T.x0n[:, _half(i)], start=True, stop=False)
        g.tensor.wait_ge(S.cut, 1)
        g.tensor.wait_ge(S.passed, lanes)
        for i, c in enumerate(HALVES):
            g.tensor.matmul(T["pn" + c][:, 0:HALF], T.eye[:], T.spn[:, _half(i)],
                            start=False, stop=True).then_inc(S["finished" + c], 1)
            g.vector.wait_ge(S["finished" + c], 1)
            g.vector.tensor_tensor(T.hn[:, _half(i)], T["pn" + c][:, 0:HALF], T.zero[:, 0:HALF],
                                   AluOpType.max).then_inc(S.hnready, 1)
        g.wait_ge(S.hnready, 2)
        sent += _send(g, T, topo, core, dst, T.hp[:], T.hn[:], S.arrived)

    src, pvia, _ = edges[(rank - 1) % n]
    g.tensor.wait_ge(S.hready, 1)
    g.tensor.wait_ge(S.arrived, _lanes(topo, src if pvia is None else pvia, core)[1])
    for i, c in enumerate(HALVES):
        g.tensor.matmul(T["py" + c][:, 0:HALF], T.hp[:], T.h[:, _half(i)],
                        start=True, stop=True).then_inc(S["multiplied" + c], 1)
        g.vector.wait_ge(S["multiplied" + c], 1)
        g.vector.tensor_copy(T.ys[:, _half(i)], T["py" + c][:, 0:HALF]).then_inc(S.rounded, 1)
    g.sync.wait_ge(S.rounded, 2)
    g.sync.dma_start(T.y[:], T.ys[:]).then_inc(S.stored, 16)
    g.sync.wait_ge(S.stored, 16)

    g.wait_ge(S.sent, sent)
